import numpy as np
import ml_dtypes

BF16 = ml_dtypes.bfloat16


def bf(x):
    return np.asarray(x, np.float32).astype(BF16)


def f32(x):
    return np.asarray(x, np.float32)


def f64(x):
    return np.asarray(x).astype(np.float64)


def striped(idx):
    return np.tile(idx.reshape(-1, 16).T, (8, 1))


S, K, M, N, E, Q = 512, 256, 256, 256, 4, 64


def setup_inputs():
    return {"base": bf(np.random.standard_normal((M, S))), "x": bf(np.random.standard_normal((K, N))), "w": bf(np.random.standard_normal((E, K, M)) / np.sqrt(K)), "b": f32(0.5 * np.random.standard_normal((M, 1))), "offs": striped(np.random.permutation(S)[:N])}


def reference(base, x, w, b, offs):
    idx = offs[:16].T.reshape(-1)
    z = f64(base).copy()
    for e in range(E):
        z[:, idx[e * Q : (e + 1) * Q]] += f64(w)[e].T @ f64(x)[:, e * Q : (e + 1) * Q]
    return z + f64(b)

@@ -1,0 +1,62 @@
+import concourse.mybir as mybir
+from concourse.masks import make_identity
+
+BF16, F32, U16 = mybir.dt.bfloat16, mybir.dt.float32, mybir.dt.uint16
+
+P = 128
+S = 512
+K = 256
+M = 256
+N = 256
+E = 4
+Q = N // E
+KB = K // P
+MB = M // P
+OFFSET_COLUMNS = Q // 16
+
+FLOPS = 2 * K * M * N
+
+
+def tile_scatter_matmul_kernel(tc, base, x, w, b, offs, out):
+    nc = tc.nc
+    with (
+        tc.tile_pool(name="held", bufs=1) as held,
+        tc.psum_pool(name="banks", bufs=1) as banks,
+    ):
+        offsets = held.tile([P, N // 16], U16, name="offsets")
+        nc.sync.dma_start(offsets[:], offs)
+
+        ident = held.tile([P, P], BF16, name="ident")
+        make_identity(nc, ident[:])
+
+        base_rows = [held.tile([P, S], BF16, name="base_rows%d" % mb) for mb in range(MB)]
+        for mb in range(MB):
+            nc.scalar.dma_start(base_rows[mb][:], base[mb * P : (mb + 1) * P, :])
+        tokens = held.tile([P, KB, N], BF16, name="tokens")
+        nc.sync.dma_start(tokens[:], x.rearrange("(kb p) n -> p kb n", p=P))
+        bias = held.tile([P, MB], F32, name="bias")
+        nc.scalar.dma_start(bias[:], b.rearrange("(mb p) o -> p (mb o)", p=P))
+        weights = [held.tile([P, KB, M], BF16, name="weights%d" % e) for e in range(E)]
+        for e in range(E):
+            queue = nc.sync if e % 2 == 0 else nc.scalar
+            queue.dma_start(weights[e][:], w[e].rearrange("(kb p) m -> p kb m", p=P))
+
+        windows = [banks.tile([P, S], F32, name="window%d" % mb) for mb in range(MB)]
+        for mb in range(MB):
+            nc.tensor.matmul(windows[mb][:], ident[:], base_rows[mb][:], start=True, stop=False)
+
+        for mb in range(MB):
+            for e in range(E):
+                places = offsets[:, e * OFFSET_COLUMNS : (e + 1) * OFFSET_COLUMNS]
+                for kb in range(KB):
+                    nc.tensor.matmul(
+                        windows[mb][:].indirect(places),
+                        weights[e][:, kb, mb * P : (mb + 1) * P],
+                        tokens[:, kb, e * Q : (e + 1) * Q],
+                        start=False,
+                        stop=(e == E - 1 and kb == KB - 1),
+                    )
+
+            result = held.tile([P, S], F32, name="result%d" % mb)
+            nc.vector.tensor_scalar_add(result[:], windows[mb][:], bias[:, mb : mb + 1])
+            nc.sync.dma_start(out[mb * P : (mb + 1) * P, :], result[:])

@@ -33,13 +33,13 @@ def tile_scatter_matmul_kernel(tc, base, x, w, b, offs, out):
         for mb in range(MB):
             nc.scalar.dma_start(base_rows[mb][:], base[mb * P : (mb + 1) * P, :])
         tokens = held.tile([P, KB, N], BF16, name="tokens")
-        nc.sync.dma_start(tokens[:], x.rearrange("(kb p) n -> p kb n", p=P))
-        bias = held.tile([P, MB], F32, name="bias")
-        nc.scalar.dma_start(bias[:], b.rearrange("(mb p) o -> p (mb o)", p=P))
+        nc.sync.dma_start(tokens[:], x.rearrange("(p kb) n -> p kb n", kb=KB))
         weights = [held.tile([P, KB, M], BF16, name="weights%d" % e) for e in range(E)]
         for e in range(E):
             queue = nc.sync if e % 2 == 0 else nc.scalar
-            queue.dma_start(weights[e][:], w[e].rearrange("(kb p) m -> p kb m", p=P))
+            queue.dma_start(weights[e][:], w[e].rearrange("(p kb) m -> p kb m", kb=KB))
+        bias = held.tile([P, MB], F32, name="bias")
+        nc.sync.dma_start(bias[:], b.rearrange("(mb p) o -> p (mb o)", p=P))
 
         windows = [banks.tile([P, S], F32, name="window%d" % mb) for mb in range(MB)]
         for mb in range(MB):
@@ -58,5 +58,9 @@ def tile_scatter_matmul_kernel(tc, base, x, w, b, offs, out):
                     )
 
             result = held.tile([P, S], F32, name="result%d" % mb)
-            nc.vector.tensor_scalar_add(result[:], windows[mb][:], bias[:, mb : mb + 1])
-            nc.sync.dma_start(out[mb * P : (mb + 1) * P, :], result[:])
+            for half, queue in enumerate((nc.sync, nc.scalar)):
+                columns = slice(half * S // 2, (half + 1) * S // 2)
+                nc.vector.tensor_scalar_add(
+                    result[:, columns], windows[mb][:, columns], bias[:, mb : mb + 1]
+                )
+                queue.dma_start(out[mb * P : (mb + 1) * P, columns], result[:, columns])

@@ -14,6 +14,8 @@ KB = K // P
 MB = M // P
 OFFSET_COLUMNS = Q // 16
 
+WARM_UP = 3
+
 FLOPS = 2 * K * M * N
 
 
@@ -28,6 +30,12 @@ def tile_scatter_matmul_kernel(tc, base, x, w, b, offs, out):
 
         ident = held.tile([P, P], BF16, name="ident")
         make_identity(nc, ident[:])
+
+        zeros = held.tile([P, S], BF16, name="zeros")
+        nc.vector.memset(zeros[:], 0.0)
+        warm = banks.tile([P, S], F32, name="warm")
+        for i in range(WARM_UP):
+            nc.tensor.matmul(warm[:], zeros[:, 0:P], zeros[:], start=True, stop=True)
 
         base_rows = [held.tile([P, S], BF16, name="base_rows%d" % mb) for mb in range(MB)]
         for mb in range(MB):

@@ -37,9 +37,8 @@ def tile_scatter_matmul_kernel(tc, base, x, w, b, offs, out):
         for i in range(WARM_UP):
             nc.tensor.matmul(warm[:], zeros[:, 0:P], zeros[:], start=True, stop=True)
 
-        base_rows = [held.tile([P, S], BF16, name="base_rows%d" % mb) for mb in range(MB)]
-        for mb in range(MB):
-            nc.scalar.dma_start(base_rows[mb][:], base[mb * P : (mb + 1) * P, :])
+        base_rows = held.tile([P, MB, S], BF16, name="base_rows")
+        nc.scalar.dma_start(base_rows[:], base.rearrange("(mb p) s -> p mb s", p=P))
         tokens = held.tile([P, KB, N], BF16, name="tokens")
         nc.sync.dma_start(tokens[:], x.rearrange("(p kb) n -> p kb n", kb=KB))
         weights = [held.tile([P, KB, M], BF16, name="weights%d" % e) for e in range(E)]
@@ -51,7 +50,7 @@ def tile_scatter_matmul_kernel(tc, base, x, w, b, offs, out):
 
         windows = [banks.tile([P, S], F32, name="window%d" % mb) for mb in range(MB)]
         for mb in range(MB):
-            nc.tensor.matmul(windows[mb][:], ident[:], base_rows[mb][:], start=True, stop=False)
+            nc.tensor.matmul(windows[mb][:], ident[:], base_rows[:, mb, :], start=True, stop=False)
 
         for mb in range(MB):
             for e in range(E):

@@ -14,8 +14,6 @@ KB = K // P
 MB = M // P
 OFFSET_COLUMNS = Q // 16
 
-WARM_UP = 3
-
 FLOPS = 2 * K * M * N
 
 
@@ -25,32 +23,25 @@ def tile_scatter_matmul_kernel(tc, base, x, w, b, offs, out):
         tc.tile_pool(name="held", bufs=1) as held,
         tc.psum_pool(name="banks", bufs=1) as banks,
     ):
-        offsets = held.tile([P, N // 16], U16, name="offsets")
-        nc.sync.dma_start(offsets[:], offs)
-
         ident = held.tile([P, P], BF16, name="ident")
         make_identity(nc, ident[:])
 
-        zeros = held.tile([P, S], BF16, name="zeros")
-        nc.vector.memset(zeros[:], 0.0)
-        warm = banks.tile([P, S], F32, name="warm")
-        for i in range(WARM_UP):
-            nc.tensor.matmul(warm[:], zeros[:, 0:P], zeros[:], start=True, stop=True)
-
-        base_rows = held.tile([P, MB, S], BF16, name="base_rows")
-        nc.scalar.dma_start(base_rows[:], base.rearrange("(mb p) s -> p mb s", p=P))
+        base_rows = [held.tile([P, S], BF16, name="base_rows%d" % mb) for mb in range(MB)]
+        for mb in range(MB):
+            nc.sync.dma_start(base_rows[mb][:], base[mb * P : (mb + 1) * P, :])
+        offsets = held.tile([P, N // 16], U16, name="offsets")
+        nc.sync.dma_start(offsets[:], offs)
         tokens = held.tile([P, KB, N], BF16, name="tokens")
         nc.sync.dma_start(tokens[:], x.rearrange("(p kb) n -> p kb n", kb=KB))
         weights = [held.tile([P, KB, M], BF16, name="weights%d" % e) for e in range(E)]
         for e in range(E):
-            queue = nc.sync if e % 2 == 0 else nc.scalar
-            queue.dma_start(weights[e][:], w[e].rearrange("(p kb) m -> p kb m", kb=KB))
+            nc.sync.dma_start(weights[e][:], w[e].rearrange("(p kb) m -> p kb m", kb=KB))
         bias = held.tile([P, MB], F32, name="bias")
         nc.sync.dma_start(bias[:], b.rearrange("(mb p) o -> p (mb o)", p=P))
 
         windows = [banks.tile([P, S], F32, name="window%d" % mb) for mb in range(MB)]
         for mb in range(MB):
-            nc.tensor.matmul(windows[mb][:], ident[:], base_rows[:, mb, :], start=True, stop=False)
+            nc.tensor.matmul(windows[mb][:], ident[:], base_rows[mb][:], start=True, stop=False)
 
         for mb in range(MB):
             for e in range(E):

@@ -43,9 +43,9 @@ def tile_scatter_matmul_kernel(tc, base, x, w, b, offs, out):
         for mb in range(MB):
             nc.tensor.matmul(windows[mb][:], ident[:], base_rows[mb][:], start=True, stop=False)
 
-        for mb in range(MB):
-            for e in range(E):
-                places = offsets[:, e * OFFSET_COLUMNS : (e + 1) * OFFSET_COLUMNS]
+        for e in range(E):
+            places = offsets[:, e * OFFSET_COLUMNS : (e + 1) * OFFSET_COLUMNS]
+            for mb in range(MB):
                 for kb in range(KB):
                     nc.tensor.matmul(
                         windows[mb][:].indirect(places),
@@ -55,6 +55,7 @@ def tile_scatter_matmul_kernel(tc, base, x, w, b, offs, out):
                         stop=(e == E - 1 and kb == KB - 1),
                     )
 
+        for mb in range(MB):
             result = held.tile([P, S], F32, name="result%d" % mb)
             for half, queue in enumerate((nc.sync, nc.scalar)):
                 columns = slice(half * S // 2, (half + 1) * S // 2)

@@ -2,6 +2,7 @@ import concourse.mybir as mybir
 from concourse.masks import make_identity
 
 BF16, F32, U16 = mybir.dt.bfloat16, mybir.dt.float32, mybir.dt.uint16
+IDENTITY = mybir.ActivationFunctionType.Identity
 
 P = 128
 S = 512
@@ -25,6 +26,9 @@ def tile_scatter_matmul_kernel(tc, base, x, w, b, offs, out):
     ):
         ident = held.tile([P, P], BF16, name="ident")
         make_identity(nc, ident[:])
+
+        primed = held.tile([P, 1], F32, name="primed")
+        nc.scalar.activation(primed[:], ident[:, 0:1], IDENTITY)
 
         base_rows = [held.tile([P, S], BF16, name="base_rows%d" % mb) for mb in range(MB)]
         for mb in range(MB):
@@ -57,9 +61,16 @@ def tile_scatter_matmul_kernel(tc, base, x, w, b, offs, out):
 
         for mb in range(MB):
             result = held.tile([P, S], F32, name="result%d" % mb)
-            for half, queue in enumerate((nc.sync, nc.scalar)):
+            for half in range(2):
                 columns = slice(half * S // 2, (half + 1) * S // 2)
-                nc.vector.tensor_scalar_add(
-                    result[:, columns], windows[mb][:, columns], bias[:, mb : mb + 1]
-                )
-                queue.dma_start(out[mb * P : (mb + 1) * P, columns], result[:, columns])
+                rows = out[mb * P : (mb + 1) * P, columns]
+                if mb == 0:
+                    nc.vector.tensor_scalar_add(
+                        result[:, columns], windows[mb][:, columns], bias[:, mb : mb + 1]
+                    )
+                    nc.sync.dma_start(rows, result[:, columns])
+                else:
+                    nc.scalar.activation(
+                        result[:, columns], windows[mb][:, columns], IDENTITY, bias=bias[:, mb : mb + 1]
+                    )
+                    nc.scalar.dma_start(rows, result[:, columns])

@@ -15,6 +15,8 @@ KB = K // P
 MB = M // P
 OFFSET_COLUMNS = Q // 16
 
+WARM_UP_MATMULS = 3
+
 FLOPS = 2 * K * M * N
 
 
@@ -24,6 +26,12 @@ def tile_scatter_matmul_kernel(tc, base, x, w, b, offs, out):
         tc.tile_pool(name="held", bufs=1) as held,
         tc.psum_pool(name="banks", bufs=1) as banks,
     ):
+        zeros = held.tile([P, S], BF16, name="zeros")
+        nc.vector.memset(zeros[:], 0.0)
+        unread = banks.tile([P, S], F32, name="unread")
+        for warm in range(WARM_UP_MATMULS):
+            nc.tensor.matmul(unread[:], zeros[:, 0:P], zeros[:], start=True, stop=True)
+
         ident = held.tile([P, P], BF16, name="ident")
         make_identity(nc, ident[:])
 

@@ -26,6 +26,9 @@ def tile_scatter_matmul_kernel(tc, base, x, w, b, offs, out):
         tc.tile_pool(name="held", bufs=1) as held,
         tc.psum_pool(name="banks", bufs=1) as banks,
     ):
+        bias_rows = held.tile([MB, P], F32, name="bias_rows")
+        nc.scalar.dma_start(bias_rows[:], b.rearrange("(mb p) o -> mb (p o)", p=P))
+
         zeros = held.tile([P, S], BF16, name="zeros")
         nc.vector.memset(zeros[:], 0.0)
         unread = banks.tile([P, S], F32, name="unread")
@@ -38,6 +41,9 @@ def tile_scatter_matmul_kernel(tc, base, x, w, b, offs, out):
         primed = held.tile([P, 1], F32, name="primed")
         nc.scalar.activation(primed[:], ident[:, 0:1], IDENTITY)
 
+        small_ident = held.tile([MB, MB], F32, name="small_ident")
+        make_identity(nc, small_ident[:])
+
         base_rows = [held.tile([P, S], BF16, name="base_rows%d" % mb) for mb in range(MB)]
         for mb in range(MB):
             nc.sync.dma_start(base_rows[mb][:], base[mb * P : (mb + 1) * P, :])
@@ -48,12 +54,15 @@ def tile_scatter_matmul_kernel(tc, base, x, w, b, offs, out):
         weights = [held.tile([P, KB, M], BF16, name="weights%d" % e) for e in range(E)]
         for e in range(E):
             nc.sync.dma_start(weights[e][:], w[e].rearrange("(p kb) m -> p kb m", kb=KB))
-        bias = held.tile([P, MB], F32, name="bias")
-        nc.sync.dma_start(bias[:], b.rearrange("(mb p) o -> p (mb o)", p=P))
 
         windows = [banks.tile([P, S], F32, name="window%d" % mb) for mb in range(MB)]
         for mb in range(MB):
             nc.tensor.matmul(windows[mb][:], ident[:], base_rows[mb][:], start=True, stop=False)
+
+        bias_bank = banks.tile([P, MB], F32, name="bias_bank")
+        nc.tensor.matmul(bias_bank[:], bias_rows[:], small_ident[:], start=True, stop=True)
+        bias = held.tile([P, MB], F32, name="bias")
+        nc.vector.tensor_copy(bias[:], bias_bank[:])
 
         for e in range(E):
             places = offsets[:, e * OFFSET_COLUMNS : (e + 1) * OFFSET_COLUMNS]

@@ -15,7 +15,7 @@ KB = K // P
 MB = M // P
 OFFSET_COLUMNS = Q // 16
 
-WARM_UP_MATMULS = 3
+WARM_UP_MATMULS = 2
 
 FLOPS = 2 * K * M * N
 
@@ -55,14 +55,14 @@ def tile_scatter_matmul_kernel(tc, base, x, w, b, offs, out):
         for e in range(E):
             nc.sync.dma_start(weights[e][:], w[e].rearrange("(p kb) m -> p kb m", kb=KB))
 
-        windows = [banks.tile([P, S], F32, name="window%d" % mb) for mb in range(MB)]
-        for mb in range(MB):
-            nc.tensor.matmul(windows[mb][:], ident[:], base_rows[mb][:], start=True, stop=False)
-
         bias_bank = banks.tile([P, MB], F32, name="bias_bank")
         nc.tensor.matmul(bias_bank[:], bias_rows[:], small_ident[:], start=True, stop=True)
         bias = held.tile([P, MB], F32, name="bias")
         nc.vector.tensor_copy(bias[:], bias_bank[:])
+
+        windows = [banks.tile([P, S], F32, name="window%d" % mb) for mb in range(MB)]
+        for mb in range(MB):
+            nc.tensor.matmul(windows[mb][:], ident[:], base_rows[mb][:], start=True, stop=False)
 
         for e in range(E):
             places = offsets[:, e * OFFSET_COLUMNS : (e + 1) * OFFSET_COLUMNS]

@@ -15,7 +15,7 @@ KB = K // P
 MB = M // P
 OFFSET_COLUMNS = Q // 16
 
-WARM_UP_MATMULS = 2
+WARM_UP_MATMULS = 8
 
 FLOPS = 2 * K * M * N
 
@@ -29,20 +29,20 @@ def tile_scatter_matmul_kernel(tc, base, x, w, b, offs, out):
         bias_rows = held.tile([MB, P], F32, name="bias_rows")
         nc.scalar.dma_start(bias_rows[:], b.rearrange("(mb p) o -> mb (p o)", p=P))
 
-        zeros = held.tile([P, S], BF16, name="zeros")
+        zeros = held.tile([P, P], BF16, name="zeros")
         nc.vector.memset(zeros[:], 0.0)
-        unread = banks.tile([P, S], F32, name="unread")
+        unread = banks.tile([P, P], F32, name="unread")
         for warm in range(WARM_UP_MATMULS):
-            nc.tensor.matmul(unread[:], zeros[:, 0:P], zeros[:], start=True, stop=True)
+            nc.tensor.matmul(unread[:], zeros[:], zeros[:], start=True, stop=True)
+
+        small_ident = held.tile([MB, MB], F32, name="small_ident")
+        make_identity(nc, small_ident[:])
 
         ident = held.tile([P, P], BF16, name="ident")
         make_identity(nc, ident[:])
 
         primed = held.tile([P, 1], F32, name="primed")
         nc.scalar.activation(primed[:], ident[:, 0:1], IDENTITY)
-
-        small_ident = held.tile([MB, MB], F32, name="small_ident")
-        make_identity(nc, small_ident[:])
 
         base_rows = [held.tile([P, S], BF16, name="base_rows%d" % mb) for mb in range(MB)]
         for mb in range(MB):

@@ -64,17 +64,17 @@ def tile_scatter_matmul_kernel(tc, base, x, w, b, offs, out):
         for mb in range(MB):
             nc.tensor.matmul(windows[mb][:], ident[:], base_rows[mb][:], start=True, stop=False)
 
-        for e in range(E):
+        order = [(0, mb) for mb in range(MB)] + [(e, mb) for mb in range(MB) for e in range(1, E)]
+        for e, mb in order:
             places = offsets[:, e * OFFSET_COLUMNS : (e + 1) * OFFSET_COLUMNS]
-            for mb in range(MB):
-                for kb in range(KB):
-                    nc.tensor.matmul(
-                        windows[mb][:].indirect(places),
-                        weights[e][:, kb, mb * P : (mb + 1) * P],
-                        tokens[:, kb, e * Q : (e + 1) * Q],
-                        start=False,
-                        stop=(e == E - 1 and kb == KB - 1),
-                    )
+            for kb in range(KB):
+                nc.tensor.matmul(
+                    windows[mb][:].indirect(places),
+                    weights[e][:, kb, mb * P : (mb + 1) * P],
+                    tokens[:, kb, e * Q : (e + 1) * Q],
+                    start=False,
+                    stop=(e == E - 1 and kb == KB - 1),
+                )
 
         for mb in range(MB):
             result = held.tile([P, S], F32, name="result%d" % mb)

@@ -81,7 +81,7 @@ def tile_scatter_matmul_kernel(tc, base, x, w, b, offs, out):
             for half in range(2):
                 columns = slice(half * S // 2, (half + 1) * S // 2)
                 rows = out[mb * P : (mb + 1) * P, columns]
-                if mb == 0:
+                if mb == MB - 1:
                     nc.vector.tensor_scalar_add(
                         result[:, columns], windows[mb][:, columns], bias[:, mb : mb + 1]
                     )

@@ -15,6 +15,8 @@ KB = K // P
 MB = M // P
 OFFSET_COLUMNS = Q // 16
 
+SMALLEST_PIECE = 64
+
 WARM_UP_MATMULS = 8
 
 FLOPS = 2 * K * M * N
@@ -78,8 +80,17 @@ def tile_scatter_matmul_kernel(tc, base, x, w, b, offs, out):
 
         for mb in range(MB):
             result = held.tile([P, S], F32, name="result%d" % mb)
-            for half in range(2):
-                columns = slice(half * S // 2, (half + 1) * S // 2)
+            if mb == MB - 1:
+                widths = []
+                while S - sum(widths) > 2 * SMALLEST_PIECE:
+                    widths.append((S - sum(widths)) // 2)
+                widths.extend([SMALLEST_PIECE, SMALLEST_PIECE])
+            else:
+                widths = [S // 2, S // 2]
+            first = 0
+            for width in widths:
+                columns = slice(first, first + width)
+                first += width
                 rows = out[mb * P : (mb + 1) * P, columns]
                 if mb == MB - 1:
                     nc.vector.tensor_scalar_add(

@@ -49,13 +49,14 @@ def tile_scatter_matmul_kernel(tc, base, x, w, b, offs, out):
         base_rows = [held.tile([P, S], BF16, name="base_rows%d" % mb) for mb in range(MB)]
         for mb in range(MB):
             nc.sync.dma_start(base_rows[mb][:], base[mb * P : (mb + 1) * P, :])
-        offsets = held.tile([P, N // 16], U16, name="offsets")
-        nc.sync.dma_start(offsets[:], offs)
         tokens = held.tile([P, KB, N], BF16, name="tokens")
         nc.sync.dma_start(tokens[:], x.rearrange("(p kb) n -> p kb n", kb=KB))
         weights = [held.tile([P, KB, M], BF16, name="weights%d" % e) for e in range(E)]
+        offsets = held.tile([P, N // 16], U16, name="offsets")
         for e in range(E):
             nc.sync.dma_start(weights[e][:], w[e].rearrange("(p kb) m -> p kb m", kb=KB))
+            if e == 0:
+                nc.sync.dma_start(offsets[:], offs)
 
         bias_bank = banks.tile([P, MB], F32, name="bias_bank")
         nc.tensor.matmul(bias_bank[:], bias_rows[:], small_ident[:], start=True, stop=True)

import concourse.mybir as mybir
from concourse.masks import make_identity

BF16, F32, U16 = mybir.dt.bfloat16, mybir.dt.float32, mybir.dt.uint16
IDENTITY = mybir.ActivationFunctionType.Identity

P = 128
S = 512
K = 256
M = 256
N = 256
E = 4
Q = N // E
KB = K // P
MB = M // P
OFFSET_COLUMNS = Q // 16

SMALLEST_PIECE = 64

WARM_UP_MATMULS = 8

FLOPS = 2 * K * M * N


def tile_scatter_matmul_kernel(tc, base, x, w, b, offs, out):
    nc = tc.nc
    with (
        tc.tile_pool(name="held", bufs=1) as held,
        tc.psum_pool(name="banks", bufs=1) as banks,
    ):
        bias_rows = held.tile([MB, P], F32, name="bias_rows")
        nc.scalar.dma_start(bias_rows[:], b.rearrange("(mb p) o -> mb (p o)", p=P))

        zeros = held.tile([P, P], BF16, name="zeros")
        nc.vector.memset(zeros[:], 0.0)
        unread = banks.tile([P, P], F32, name="unread")
        for warm in range(WARM_UP_MATMULS):
            nc.tensor.matmul(unread[:], zeros[:], zeros[:], start=True, stop=True)

        small_ident = held.tile([MB, MB], F32, name="small_ident")
        make_identity(nc, small_ident[:])

        ident = held.tile([P, P], BF16, name="ident")
        make_identity(nc, ident[:])

        primed = held.tile([P, 1], F32, name="primed")
        nc.scalar.activation(primed[:], ident[:, 0:1], IDENTITY)

        base_rows = [held.tile([P, S], BF16, name="base_rows%d" % mb) for mb in range(MB)]
        for mb in range(MB):
            nc.sync.dma_start(base_rows[mb][:], base[mb * P : (mb + 1) * P, :])
        tokens = held.tile([P, KB, N], BF16, name="tokens")
        nc.sync.dma_start(tokens[:], x.rearrange("(p kb) n -> p kb n", kb=KB))
        weights = [held.tile([P, KB, M], BF16, name="weights%d" % e) for e in range(E)]
        offsets = held.tile([P, N // 16], U16, name="offsets")
        for e in range(E):
            nc.sync.dma_start(weights[e][:], w[e].rearrange("(p kb) m -> p kb m", kb=KB))
            if e == 0:
                nc.sync.dma_start(offsets[:], offs)

        bias_bank = banks.tile([P, MB], F32, name="bias_bank")
        nc.tensor.matmul(bias_bank[:], bias_rows[:], small_ident[:], start=True, stop=True)
        bias = held.tile([P, MB], F32, name="bias")
        nc.vector.tensor_copy(bias[:], bias_bank[:])

        windows = [banks.tile([P, S], F32, name="window%d" % mb) for mb in range(MB)]
        for mb in range(MB):
            nc.tensor.matmul(windows[mb][:], ident[:], base_rows[mb][:], start=True, stop=False)

        order = [(0, mb) for mb in range(MB)] + [(e, mb) for mb in range(MB) for e in range(1, E)]
        for e, mb in order:
            places = offsets[:, e * OFFSET_COLUMNS : (e + 1) * OFFSET_COLUMNS]
            for kb in range(KB):
                nc.tensor.matmul(
                    windows[mb][:].indirect(places),
                    weights[e][:, kb, mb * P : (mb + 1) * P],
                    tokens[:, kb, e * Q : (e + 1) * Q],
                    start=False,
                    stop=(e == E - 1 and kb == KB - 1),
                )

        for mb in range(MB):
            result = held.tile([P, S], F32, name="result%d" % mb)
            if mb == MB - 1:
                widths = []
                while S - sum(widths) > 2 * SMALLEST_PIECE:
                    widths.append((S - sum(widths)) // 2)
                widths.extend([SMALLEST_PIECE, SMALLEST_PIECE])
            else:
                widths = [S // 2, S // 2]
            first = 0
            for width in widths:
                columns = slice(first, first + width)
                first += width
                rows = out[mb * P : (mb + 1) * P, columns]
                if mb == MB - 1:
                    nc.vector.tensor_scalar_add(
                        result[:, columns], windows[mb][:, columns], bias[:, mb : mb + 1]
                    )
                    nc.sync.dma_start(rows, result[:, columns])
                else:
                    nc.scalar.activation(
                        result[:, columns], windows[mb][:, columns], IDENTITY, bias=bias[:, mb : mb + 1]
                    )
                    nc.scalar.dma_start(rows, result[:, columns])
